import numpy as np
import ml_dtypes


def mxq(x, axis, fmt="e4m3"):
    dtype, down = {"e4m3": (ml_dtypes.float8_e4m3fn, 7), "e5m2": (ml_dtypes.float8_e5m2, 14)}[fmt]
    v = np.moveaxis(np.asarray(x, np.float32).astype(ml_dtypes.bfloat16).astype(np.float64), axis, -1)
    blocks = v.reshape(v.shape[:-1] + (-1, 32))
    amax = np.abs(blocks).max(-1, keepdims=True)
    byte = np.maximum(np.where(amax > 0, np.frexp(amax)[1] - 1 + 127, 0) - down, 1)
    scale = np.exp2(byte - 127.0)
    codes = (blocks / scale).astype(np.float32).astype(dtype).astype(np.float64)
    return np.moveaxis((codes * scale).reshape(v.shape), -1, axis)


WIDE = False


def mx_kscale(k):
    if not WIDE:
        return np.ones(k)
    levels = np.array([10, -10, 5, -5, 0])
    if k % 512:
        return np.exp2(np.random.permutation(np.resize(levels, k // 32))).repeat(32)
    a = np.empty((k // 512, 16))
    for p in range(k // 512):
        a[p, :8] = np.random.permutation(np.resize(levels, 8))
        for g in range(8):
            far = levels[np.abs(levels - a[p, g]) >= 10]
            a[p, g + 8] = far[np.random.randint(len(far))]
    return np.exp2(a.ravel()).repeat(32)


def f64(x):
    return np.asarray(x).astype(np.float64)


def striped(idx):
    return np.tile(idx.reshape(-1, 16).T, (8, 1)).astype(np.uint16)


def unstriped(offs):
    return offs[:16].T.reshape(-1).astype(np.int64)


def relu(v):
    return np.maximum(v, 0.0)


K, T, D, S, V, N = 1024, 1024, 8, 4096, 512, 128


def setup_inputs():
    n = np.random.standard_normal
    s = mx_kscale(K)[:, None]
    return {
        "xT": (n((K, T)) * s).astype(np.float32),
        "w": (n((K, N)) / np.sqrt(K) / s).astype(np.float32),
        "b": (0.3 * n((N, 1))).astype(np.float32),
        "offs": striped(np.concatenate([np.random.permutation(T)[:V] for _ in range(D)])),
    }


def reference(xT, w, b, offs):
    idx = unstriped(offs)
    x = np.empty((K, V))
    for l in range(D):
        r = l // 4 * (4 * K // D) + l % 4 + 4 * np.arange(K // D)
        x[r] = f64(xT)[r][:, idx[l * V:(l + 1) * V]]
    xq = mxq(x, 0, "e4m3")
    return relu((mxq(f64(w), 0, "e4m3").T @ xq) + f64(b))

from contextlib import ExitStack

import concourse.mybir as mybir

K, T, D, V, N = 1024, 1024, 8, 512, 128
FLOPS = 2 * K * N * V
F32 = mybir.dt.float32
BF16 = mybir.dt.bfloat16
U32 = mybir.dt.uint32
U16 = mybir.dt.uint16
U8 = mybir.dt.uint8
FP8X4 = mybir.dt.float8_e4m3fn_x4
COPY = mybir.ActivationFunctionType.Copy
RELU = mybir.ActivationFunctionType.Relu
MULT, ADD, MAX = mybir.AluOpType.mult, mybir.AluOpType.add, mybir.AluOpType.max
P = 128


def tile_picked_grid_lin_relu_sub_l_kernel(tc, xT, w, b, offs, out):
    nc = tc.nc
    with ExitStack() as ctx:
        keep = ctx.enter_context(tc.tile_pool(name="keep", bufs=1))
        psum = ctx.enter_context(tc.psum_pool(name="psum", bufs=1))
        offsets = keep.tile([P, D * V // 16], U16, name="offsets")
        nc.sync.dma_start(offsets[:], offs)
        bias = keep.tile([P, 1], F32, name="bias")
        warm = keep.tile([P, 1], F32, name="warm")
        warm2 = keep.tile([P, 1], F32, name="warm2")
        xrows = xT.rearrange("(g p j) c -> g j p c", g=2, j=4)
        wrows = w.rearrange("(g p j) m -> g p j m", g=2, j=4)
        tables = {}
        for l in range(D):
            tables[l] = keep.tile([P, T], F32, name="table%d" % l)
        wraw = keep.tile([P, 2, 4, N], F32, name="wraw")
        wg = keep.tile([P, 2, N, 4], BF16, name="wg", align_bytes=64)
        wcodes = keep.tile([P, 2, N], U32, name="wcodes", align_bytes=64)
        wscales = keep.tile([P, 2, N], U8, name="wscales", align_bytes=64)
        g4 = {}
        grouped = {}
        codes = {}
        scales = {}
        for g in (0, 1):
            g4[g] = keep.tile([P, 4, V], F32, name="g4_%d" % g)
            grouped[g] = keep.tile([P, V, 4], BF16, name="grouped%d" % g, align_bytes=64)
            codes[g] = keep.tile([P, V], U32, name="codes%d" % g, align_bytes=64)
            scales[g] = keep.tile([P, V], U8, name="scales%d" % g, align_bytes=64)
        banks = [psum.tile([P, 512], F32, name="bank%d" % c) for c in range(4)]
        res = keep.tile([P, V], F32, name="res")
        win = {}

        def load(l):
            nc.sync.dma_start(tables[l][:], xrows[l // 4, l % 4])

        def loadw(g):
            nc.sync.dma_start(wraw[:, g], wrows[g])

        def look(l, lo, hi):
            return offsets[:, (l * V + lo) // 16 : (l * V + hi) // 16]

        def move(eng, dst, src):
            if eng == "s":
                nc.scalar.copy(dst, src)
            elif eng == "g":
                nc.gpsimd.tensor_scalar(dst, src, 1.0, 0.0, MULT, ADD)
            else:
                nc.vector.tensor_copy(dst, src)

        def ga(l, lo=0, hi=V):
            nc.vector.tensor_copy(g4[l // 4][:, l % 4, lo:hi], tables[l][:].indirect(look(l, lo, hi)))

        def gb(l, lo=0, hi=V):
            nc.vector.tensor_copy(grouped[l // 4][:, lo:hi, l % 4], tables[l][:].indirect(look(l, lo, hi)))

        def cast(eng, l):
            win[l] = keep.tile([P, T], BF16, name="win%d" % l)
            move(eng, win[l][:], tables[l][:])

        def gf(l, lo=0, hi=V):
            nc.scalar.activation(grouped[l // 4][:, lo:hi, l % 4], win[l][:].indirect(look(l, lo, hi)), COPY)

        def inter(eng, g, lo, hi, t0=0, t1=4):
            move(eng, grouped[g][:, lo:hi, t0:t1], g4[g][:, t0:t1, lo:hi].rearrange("p t n -> p n t"))

        def q(g, lo=0, hi=V):
            nc.vector.quantize_mx(out=codes[g][:, lo:hi].bitcast(FP8X4), scales=scales[g][:, lo:hi],
                                  in_=grouped[g][:, lo:hi, :].rearrange("p n j -> p (n j)"))

        def wcopy(eng, g):
            move(eng, wg[:, g], wraw[:, g].rearrange("p j m -> p m j"))

        def wq(g):
            nc.vector.quantize_mx(out=wcodes[:, g].bitcast(FP8X4), scales=wscales[:, g],
                                  in_=wg[:, g].rearrange("p m j -> p (m j)"))

        def mm(g, bank, lo, hi, start, stop):
            nc.tensor.matmul_mx(out=banks[bank][:, 0 : hi - lo], lhsT=wcodes[:, g].bitcast(FP8X4), lhsT_scale=wscales[:, g],
                                rhs=codes[g][:, lo:hi].bitcast(FP8X4), rhs_scale=scales[g][:, lo:hi],
                                start=start, stop=stop)

        def fin(eng, bank, lo, hi, dma):
            if eng == "s":
                nc.scalar.activation(res[:, lo:hi], banks[bank][:, 0 : hi - lo], RELU, bias=bias[:])
            else:
                nc.vector.tensor_scalar(res[:, lo:hi], banks[bank][:, 0 : hi - lo], bias[:], 0.0, ADD, MAX)
            (nc.sync if dma == "y" else nc.scalar).dma_start(out[:, lo:hi], res[:, lo:hi])

        nc.vector.memset(warm[:], 0.0)
        nc.scalar.activation(warm2[:], warm[:], RELU)
        nc.scalar.dma_start(bias[:], b)
        load(0)
        load(2)
        load(1)
        load(3)
        load(4)
        load(6)
        load(5)
        load(7)
        loadw(0)
        loadw(1)
        cast("g", 0)
        gf(0)
        gb(2)
        cast("g", 1)
        gf(1)
        gb(3)
        cast("g", 4)
        gf(4)
        q(0)
        gb(6)
        cast("v", 5)
        gf(5)
        gb(7, 0, 256)
        wcopy("g", 0)
        wq(0)
        wcopy("s", 1)
        gb(7, 256, 512)
        mm(0, 0, 0, 256, True, False)
        mm(0, 1, 256, 512, True, False)
        q(1, 0, 256)
        wq(1)
        mm(1, 0, 0, 256, False, True)
        fin("s", 0, 0, 256, "y")
        q(1, 256, 512)
        mm(1, 1, 256, 512, False, True)
        fin("v", 1, 256, 512, "s")
